import numpy as np
import ml_dtypes


def mxq(x, axis, fmt="e4m3"):
    dtype, down = {"e4m3": (ml_dtypes.float8_e4m3fn, 7), "e5m2": (ml_dtypes.float8_e5m2, 14)}[fmt]
    v = np.moveaxis(np.asarray(x, np.float32).astype(ml_dtypes.bfloat16).astype(np.float64), axis, -1)
    blocks = v.reshape(v.shape[:-1] + (-1, 32))
    amax = np.abs(blocks).max(-1, keepdims=True)
    byte = np.maximum(np.where(amax > 0, np.frexp(amax)[1] - 1 + 127, 0) - down, 1)
    scale = np.exp2(byte - 127.0)
    codes = (blocks / scale).astype(np.float32).astype(dtype).astype(np.float64)
    return np.moveaxis((codes * scale).reshape(v.shape), -1, axis)


WIDE = False


def mx_kscale(k):
    if not WIDE:
        return np.ones(k)
    levels = np.array([10, -10, 5, -5, 0])
    if k % 512:
        return np.exp2(np.random.permutation(np.resize(levels, k // 32))).repeat(32)
    a = np.empty((k // 512, 16))
    for p in range(k // 512):
        a[p, :8] = np.random.permutation(np.resize(levels, 8))
        for g in range(8):
            far = levels[np.abs(levels - a[p, g]) >= 10]
            a[p, g + 8] = far[np.random.randint(len(far))]
    return np.exp2(a.ravel()).repeat(32)


def f64(x):
    return np.asarray(x).astype(np.float64)


def striped(idx):
    return np.tile(idx.reshape(-1, 16).T, (8, 1)).astype(np.uint16)


def unstriped(offs):
    return offs[:16].T.reshape(-1).astype(np.int64)


E2M1 = np.array([0.0, 0.5, 1.0, 1.5, 2.0, 3.0, 4.0, 6.0, -0.0, -0.5, -1.0, -1.5, -2.0, -3.0, -4.0, -6.0])


def pack_weight(w, fmt):
    k, n = w.shape
    w = f64(np.asarray(w, np.float32).astype(ml_dtypes.bfloat16)).reshape(k // 32, 32, n)
    amax = np.abs(w).max(1)
    if fmt == "e4m3":
        byte = np.frexp(amax)[1] - 1 + 127 - 7
    else:
        mant, ex = np.frexp(amax / 6.0)
        byte = np.where(mant > 0.5, ex, ex - 1) + 127
    byte = np.clip(np.where(amax > 0, byte, 1), 1, 254)
    scaled = (w * np.exp2(127.0 - byte)[:, None, :]).reshape(k, n).astype(np.float32)
    by_word = np.ascontiguousarray(scaled.reshape(k // 512, 128, 4, n).transpose(0, 1, 3, 2))
    if fmt == "e4m3":
        words = by_word.astype(ml_dtypes.float8_e4m3fn).view(np.uint8)
    else:
        c = by_word.astype(ml_dtypes.float4_e2m1fn).view(np.uint8) & 0xF
        words = (c[..., 0::2] | (c[..., 1::2] << 4)).reshape(k // 512, 128, 2 * n)
    return np.ascontiguousarray(words), np.ascontiguousarray(byte.astype(np.uint8).reshape(k // 512, 16, n))


def unpack_weight(words, scales, fmt):
    g, _, n = scales.shape
    words = np.ascontiguousarray(words).reshape(g, 128, n, -1)
    if fmt == "e4m3":
        vals = words.view(ml_dtypes.float8_e4m3fn).astype(np.float64)
    else:
        nib = np.empty((g, 128, n, 4), np.uint8)
        nib[..., 0::2] = words & 0xF
        nib[..., 1::2] = words >> 4
        vals = E2M1[nib]
    vals = vals * np.repeat(np.exp2(scales.astype(np.float64) - 127.0), 8, axis=1)[..., None]
    return vals.transpose(0, 1, 3, 2).reshape(g * 512, n)


def pack_table(v):
    words, scales = pack_weight(v, "e4m3")
    return np.concatenate([words.reshape(words.shape[0], -1), scales.reshape(scales.shape[0], -1)], axis=1)


def unpack_table(tab):
    g, t = tab.shape[0], tab.shape[1] // 528
    return unpack_weight(tab[:, :512 * t].reshape(g, 128, t, 4), tab[:, 512 * t:].reshape(g, 16, t), "e4m3")


K, H, M, T, S = 512, 512, 1024, 2048, 512


def setup_inputs():
    n = np.random.standard_normal
    s = mx_kscale(K)[:, None]
    u = mx_kscale(H)[:, None]
    p_w2 = pack_weight(1.4 * n((H, M)) / np.sqrt(H) / u, "e2m1")
    return {
        "tab": pack_table(n((K, T)) * s),
        "w1": (n((K, H)) / np.sqrt(K) / s * u.T).astype(np.float32),
        "w2_words": p_w2[0],
        "w2_scales": p_w2[1],
        "b": (0.3 * n(1024)).astype(np.float32),
        "offs": striped(np.random.permutation(T)[:S]),
    }


def reference(tab, w1, w2_words, w2_scales, b, offs):
    tab_ = unpack_table(tab)[:, unstriped(offs)]
    w1_ = mxq(f64(w1), 0, "e4m3")
    w2_ = unpack_weight(w2_words, w2_scales, "e2m1")
    h_ = mxq(np.maximum(w1_.T @ tab_, 0.0), 0, "e4m3")
    y = h_.T @ w2_
    return y + f64(b)[None, :]

@@ -1,0 +1,151 @@
+from contextlib import ExitStack
+
+import concourse.mybir as mybir
+from concourse.masks import make_identity
+
+K, H, M, T, S = 512, 512, 1024, 2048, 512
+FLOPS = 2 * K * H * S + 2 * H * M * S
+
+P = 128
+F32 = mybir.dt.float32
+BF16 = mybir.dt.bfloat16
+I32 = mybir.dt.int32
+U32 = mybir.dt.uint32
+U16 = mybir.dt.uint16
+U8 = mybir.dt.uint8
+FP8X4 = mybir.dt.float8_e4m3fn_x4
+FP4X4 = mybir.dt.float4_e2m1fn_x4
+COPY = mybir.ActivationFunctionType.Copy
+RELU = mybir.ActivationFunctionType.Relu
+ADD = mybir.AluOpType.add
+
+W1_VECTOR = 80
+
+
+def tile_list_tabmlp_tm_bias_kernel(tc, tab, w1, w2_words, w2_scales, b, offs, out):
+    nc = tc.nc
+    with ExitStack() as ctx:
+        keep = ctx.enter_context(tc.tile_pool(name="keep", bufs=1))
+        ring = ctx.enter_context(tc.tile_pool(name="ring", bufs=4))
+        outs = ctx.enter_context(tc.tile_pool(name="outs", bufs=8))
+        psum = ctx.enter_context(tc.psum_pool(name="psum", bufs=8))
+
+        offsets = keep.tile([P, S // 16], U16, name="offsets")
+        b_col = keep.tile([P, 8], F32, name="b_col")
+        tab_words = keep.tile([P, T], U32, name="tab_words", align_bytes=64)
+        tab_scales = keep.tile([P, T], U8, name="tab_scales", align_bytes=64)
+        w1_raw = keep.tile([P, 4, H], F32, name="w1_raw", align_bytes=64)
+        w2_codes = keep.tile([P, 2 * M], U8, name="w2_codes", align_bytes=64)
+        w2_sc = keep.tile([P, M], U8, name="w2_sc", align_bytes=64)
+
+        nc.vector.memset(tab_scales[:].bitcast(I32), 0)
+        nc.vector.memset(w2_sc[:].bitcast(I32), 0)
+
+        nc.sync.dma_start(offsets[:], offs)
+        nc.scalar.dma_start(out=b_col[:], in_=b.rearrange("(n c) -> n c", c=8))
+        nc.sync.dma_start(out=w1_raw[:], in_=w1.rearrange("(p j) r -> p j r", j=4))
+        scales_dram = tab[0, 512 * T : 528 * T].rearrange("(q t) -> q t", q=16)
+        for q in range(4):
+            nc.sync.dma_start(
+                out=tab_scales[32 * q : 32 * q + 4, :].bitcast(I32),
+                in_=scales_dram[4 * q : 4 * q + 4, :].bitcast(I32),
+            )
+        words_dram = tab[0, 0 : 512 * T].rearrange("(p b) -> p b", p=P)
+        nc.sync.dma_start(out=tab_words[:].bitcast(I32), in_=words_dram.bitcast(I32))
+        nc.sync.dma_start(out=w2_codes[:].bitcast(I32), in_=w2_words[0].bitcast(I32))
+        for q in range(4):
+            nc.sync.dma_start(
+                out=w2_sc[32 * q : 32 * q + 4, :].bitcast(I32),
+                in_=w2_scales[0, 4 * q : 4 * q + 4, :].bitcast(I32),
+            )
+
+        ident = keep.tile([P, P], F32, name="ident")
+        make_identity(nc, ident[:])
+        bias = keep.tile([P, M], F32, name="bias")
+        bias_v = bias[:].rearrange("p (n u c) -> p u n c", u=2, c=4)
+        for u in range(2):
+            bank = psum.tile([P, 512], F32, name="bank")
+            for c in range(4):
+                column = b_col[:, 4 * u + c : 4 * u + c + 1].to_broadcast([P, P])
+                nc.tensor.transpose(bank[:, 128 * c : 128 * c + 128], column, ident[:])
+            nc.scalar.activation(bias_v[:, u], bank[:].rearrange("p (c n) -> p n c", c=4), COPY)
+
+        x_scales = keep.tile([P, S], U8, name="x_scales", align_bytes=64)
+        nc.vector.tensor_copy(x_scales[:], tab_scales[:].indirect(offsets[:]))
+
+        w1_bf = keep.tile([P, 4 * H], BF16, name="w1_bf", align_bytes=64)
+        w1_dst = w1_bf[:].rearrange("p (t m j) -> p m t j", t=4, j=4)
+        w1_src = w1_raw[:].rearrange("p j (m t) -> p m t j", t=4)
+        nc.vector.tensor_copy(out=w1_dst[:, :W1_VECTOR], in_=w1_src[:, :W1_VECTOR])
+        nc.scalar.activation(w1_dst[:, W1_VECTOR:], w1_src[:, W1_VECTOR:], COPY)
+        w1_codes = keep.tile([P, H], U32, name="w1_codes", align_bytes=64)
+        w1_sc = keep.tile([P, H], U8, name="w1_sc", align_bytes=64)
+        nc.vector.quantize_mx(out=w1_codes[:].bitcast(FP8X4), scales=w1_sc[:], in_=w1_bf[:])
+
+        x_words = []
+        for g in range(2):
+            words = keep.tile([P, 256], U32, name=f"x_words{g}", align_bytes=64)
+            nc.vector.tensor_copy(words[:], tab_words[:].indirect(offsets[:, 16 * g : 16 * g + 16]))
+            x_words.append(words)
+
+        h_banks, h_codes = [], []
+
+        def first_product(c):
+            bank = psum.tile([P, 512], F32, name="bank")
+            cols = slice(128 * (c % 2), 128 * (c % 2) + 128)
+            for t in range(4):
+                r = slice(128 * t, 128 * t + 128)
+                nc.tensor.matmul_mx(
+                    out=bank[:, r],
+                    lhsT=w1_codes[:, r].bitcast(FP8X4),
+                    lhsT_scale=w1_sc[:, r],
+                    rhs=x_words[c // 2][:, cols].bitcast(FP8X4),
+                    rhs_scale=x_scales[:, 128 * c : 128 * c + 128],
+                    start=True,
+                    stop=True,
+                )
+            h_bf = ring.tile([P, 512], BF16, name="h_bf", align_bytes=64)
+            nc.scalar.activation(
+                h_bf[:].rearrange("p (n t) -> p n t", t=4), bank[:].rearrange("p (t n) -> p n t", t=4), RELU
+            )
+            h_banks.append(h_bf)
+
+        def quantise(c):
+            codes = ring.tile([P, 128], U32, name="h_codes", align_bytes=64)
+            scales = ring.tile([P, 128], U8, name="h_scales", align_bytes=64)
+            nc.vector.quantize_mx(out=codes[:].bitcast(FP8X4), scales=scales[:], in_=h_banks[c][:])
+            h_codes.append((codes, scales))
+
+        def second_product(c, n):
+            codes, scales = h_codes[c]
+            bank = psum.tile([P, 512], F32, name="bank")
+            nc.tensor.matmul_mx(
+                out=bank[:],
+                lhsT=codes[:].bitcast(FP8X4),
+                lhsT_scale=scales[:],
+                rhs=w2_codes[:, 1024 * n : 1024 * n + 1024].bitcast(FP4X4),
+                rhs_scale=w2_sc[:, 512 * n : 512 * n + 512],
+                start=True,
+                stop=True,
+            )
+            result = outs.tile([P, 512], F32, name="result")
+            cols = slice(512 * n, 512 * n + 512)
+            nc.vector.tensor_tensor(result[:], bank[:], bias[:, cols], ADD)
+            nc.sync.dma_start(out=out[128 * c : 128 * c + 128, cols], in_=result[:])
+
+        first_product(0)
+        first_product(1)
+        quantise(0)
+        second_product(0, 0)
+        first_product(2)
+        quantise(1)
+        second_product(0, 1)
+        second_product(1, 0)
+        first_product(3)
+        quantise(2)
+        second_product(1, 1)
+        second_product(2, 0)
+        quantise(3)
+        second_product(2, 1)
+        second_product(3, 0)
+        second_product(3, 1)

@@ -19,7 +19,7 @@ COPY = mybir.ActivationFunctionType.Copy
 RELU = mybir.ActivationFunctionType.Relu
 ADD = mybir.AluOpType.add
 
-W1_VECTOR = 80
+W1_VECTOR = 64
 
 
 def tile_list_tabmlp_tm_bias_kernel(tc, tab, w1, w2_words, w2_scales, b, offs, out):
@@ -27,7 +27,7 @@ def tile_list_tabmlp_tm_bias_kernel(tc, tab, w1, w2_words, w2_scales, b, offs, o
     with ExitStack() as ctx:
         keep = ctx.enter_context(tc.tile_pool(name="keep", bufs=1))
         ring = ctx.enter_context(tc.tile_pool(name="ring", bufs=4))
-        outs = ctx.enter_context(tc.tile_pool(name="outs", bufs=8))
+        outs = ctx.enter_context(tc.tile_pool(name="outs", bufs=9))
         psum = ctx.enter_context(tc.psum_pool(name="psum", bufs=8))
 
         offsets = keep.tile([P, S // 16], U16, name="offsets")
@@ -39,7 +39,7 @@ def tile_list_tabmlp_tm_bias_kernel(tc, tab, w1, w2_words, w2_scales, b, offs, o
         w2_sc = keep.tile([P, M], U8, name="w2_sc", align_bytes=64)
 
         nc.vector.memset(tab_scales[:].bitcast(I32), 0)
-        nc.vector.memset(w2_sc[:].bitcast(I32), 0)
+        nc.gpsimd.memset(w2_sc[:].bitcast(I32), 0)
 
         nc.sync.dma_start(offsets[:], offs)
         nc.scalar.dma_start(out=b_col[:], in_=b.rearrange("(n c) -> n c", c=8))
@@ -70,8 +70,12 @@ def tile_list_tabmlp_tm_bias_kernel(tc, tab, w1, w2_words, w2_scales, b, offs, o
                 nc.tensor.transpose(bank[:, 128 * c : 128 * c + 128], column, ident[:])
             nc.scalar.activation(bias_v[:, u], bank[:].rearrange("p (c n) -> p n c", c=4), COPY)
 
-        x_scales = keep.tile([P, S], U8, name="x_scales", align_bytes=64)
-        nc.vector.tensor_copy(x_scales[:], tab_scales[:].indirect(offsets[:]))
+        x_scales = []
+
+        def gather_scales(g):
+            scales = keep.tile([P, 256], U8, name=f"x_scales{g}", align_bytes=64)
+            nc.vector.tensor_copy(scales[:], tab_scales[:].indirect(offsets[:, 16 * g : 16 * g + 16]))
+            x_scales.append(scales)
 
         w1_bf = keep.tile([P, 4 * H], BF16, name="w1_bf", align_bytes=64)
         w1_dst = w1_bf[:].rearrange("p (t m j) -> p m t j", t=4, j=4)
@@ -80,6 +84,7 @@ def tile_list_tabmlp_tm_bias_kernel(tc, tab, w1, w2_words, w2_scales, b, offs, o
         nc.scalar.activation(w1_dst[:, W1_VECTOR:], w1_src[:, W1_VECTOR:], COPY)
         w1_codes = keep.tile([P, H], U32, name="w1_codes", align_bytes=64)
         w1_sc = keep.tile([P, H], U8, name="w1_sc", align_bytes=64)
+        gather_scales(0)
         nc.vector.quantize_mx(out=w1_codes[:].bitcast(FP8X4), scales=w1_sc[:], in_=w1_bf[:])
 
         x_words = []
@@ -87,6 +92,8 @@ def tile_list_tabmlp_tm_bias_kernel(tc, tab, w1, w2_words, w2_scales, b, offs, o
             words = keep.tile([P, 256], U32, name=f"x_words{g}", align_bytes=64)
             nc.vector.tensor_copy(words[:], tab_words[:].indirect(offsets[:, 16 * g : 16 * g + 16]))
             x_words.append(words)
+
+        gather_scales(1)
 
         h_banks, h_codes = [], []
 
@@ -100,7 +107,7 @@ def tile_list_tabmlp_tm_bias_kernel(tc, tab, w1, w2_words, w2_scales, b, offs, o
                     lhsT=w1_codes[:, r].bitcast(FP8X4),
                     lhsT_scale=w1_sc[:, r],
                     rhs=x_words[c // 2][:, cols].bitcast(FP8X4),
-                    rhs_scale=x_scales[:, 128 * c : 128 * c + 128],
+                    rhs_scale=x_scales[c // 2][:, cols],
                     start=True,
                     stop=True,
                 )
@@ -116,36 +123,41 @@ def tile_list_tabmlp_tm_bias_kernel(tc, tab, w1, w2_words, w2_scales, b, offs, o
             nc.vector.quantize_mx(out=codes[:].bitcast(FP8X4), scales=scales[:], in_=h_banks[c][:])
             h_codes.append((codes, scales))
 
-        def second_product(c, n):
+        def second_product(c, n0, width, on_gpsimd=False):
             codes, scales = h_codes[c]
             bank = psum.tile([P, 512], F32, name="bank")
+            cols = slice(n0, n0 + width)
             nc.tensor.matmul_mx(
-                out=bank[:],
+                out=bank[:, :width],
                 lhsT=codes[:].bitcast(FP8X4),
                 lhsT_scale=scales[:],
-                rhs=w2_codes[:, 1024 * n : 1024 * n + 1024].bitcast(FP4X4),
-                rhs_scale=w2_sc[:, 512 * n : 512 * n + 512],
+                rhs=w2_codes[:, 2 * n0 : 2 * (n0 + width)].bitcast(FP4X4),
+                rhs_scale=w2_sc[:, cols],
                 start=True,
                 stop=True,
             )
             result = outs.tile([P, 512], F32, name="result")
-            cols = slice(512 * n, 512 * n + 512)
-            nc.vector.tensor_tensor(result[:], bank[:], bias[:, cols], ADD)
-            nc.sync.dma_start(out=out[128 * c : 128 * c + 128, cols], in_=result[:])
+            if on_gpsimd:
+                nc.scalar.activation(result[:, :width], bank[:, :width], COPY)
+                nc.gpsimd.tensor_tensor(result[:, :width], result[:, :width], bias[:, cols], ADD)
+            else:
+                nc.vector.tensor_tensor(result[:, :width], bank[:, :width], bias[:, cols], ADD)
+            nc.sync.dma_start(out=out[128 * c : 128 * c + 128, cols], in_=result[:, :width])
 
         first_product(0)
         first_product(1)
         quantise(0)
-        second_product(0, 0)
+        second_product(0, 0, 256)
+        second_product(0, 256, 256)
         first_product(2)
         quantise(1)
-        second_product(0, 1)
-        second_product(1, 0)
+        second_product(0, 512, 512, on_gpsimd=True)
         first_product(3)
+        second_product(1, 0, 512)
         quantise(2)
-        second_product(1, 1)
-        second_product(2, 0)
+        second_product(1, 512, 512)
+        second_product(2, 0, 512)
         quantise(3)
-        second_product(2, 1)
-        second_product(3, 0)
-        second_product(3, 1)
+        second_product(2, 512, 512, on_gpsimd=True)
+        second_product(3, 0, 512)
+        second_product(3, 512, 512)

from contextlib import ExitStack

import concourse.mybir as mybir
from concourse.masks import make_identity

K, H, M, T, S = 512, 512, 1024, 2048, 512
FLOPS = 2 * K * H * S + 2 * H * M * S

P = 128
F32 = mybir.dt.float32
BF16 = mybir.dt.bfloat16
I32 = mybir.dt.int32
U32 = mybir.dt.uint32
U16 = mybir.dt.uint16
U8 = mybir.dt.uint8
FP8X4 = mybir.dt.float8_e4m3fn_x4
FP4X4 = mybir.dt.float4_e2m1fn_x4
COPY = mybir.ActivationFunctionType.Copy
RELU = mybir.ActivationFunctionType.Relu
ADD = mybir.AluOpType.add

W1_VECTOR = 64


def tile_list_tabmlp_tm_bias_kernel(tc, tab, w1, w2_words, w2_scales, b, offs, out):
    nc = tc.nc
    with ExitStack() as ctx:
        keep = ctx.enter_context(tc.tile_pool(name="keep", bufs=1))
        ring = ctx.enter_context(tc.tile_pool(name="ring", bufs=4))
        outs = ctx.enter_context(tc.tile_pool(name="outs", bufs=9))
        psum = ctx.enter_context(tc.psum_pool(name="psum", bufs=8))

        offsets = keep.tile([P, S // 16], U16, name="offsets")
        b_col = keep.tile([P, 8], F32, name="b_col")
        tab_words = keep.tile([P, T], U32, name="tab_words", align_bytes=64)
        tab_scales = keep.tile([P, T], U8, name="tab_scales", align_bytes=64)
        w1_raw = keep.tile([P, 4, H], F32, name="w1_raw", align_bytes=64)
        w2_codes = keep.tile([P, 2 * M], U8, name="w2_codes", align_bytes=64)
        w2_sc = keep.tile([P, M], U8, name="w2_sc", align_bytes=64)

        nc.vector.memset(tab_scales[:].bitcast(I32), 0)
        nc.gpsimd.memset(w2_sc[:].bitcast(I32), 0)

        nc.sync.dma_start(offsets[:], offs)
        nc.scalar.dma_start(out=b_col[:], in_=b.rearrange("(n c) -> n c", c=8))
        nc.sync.dma_start(out=w1_raw[:], in_=w1.rearrange("(p j) r -> p j r", j=4))
        scales_dram = tab[0, 512 * T : 528 * T].rearrange("(q t) -> q t", q=16)
        for q in range(4):
            nc.sync.dma_start(
                out=tab_scales[32 * q : 32 * q + 4, :].bitcast(I32),
                in_=scales_dram[4 * q : 4 * q + 4, :].bitcast(I32),
            )
        words_dram = tab[0, 0 : 512 * T].rearrange("(p b) -> p b", p=P)
        nc.sync.dma_start(out=tab_words[:].bitcast(I32), in_=words_dram.bitcast(I32))
        nc.sync.dma_start(out=w2_codes[:].bitcast(I32), in_=w2_words[0].bitcast(I32))
        for q in range(4):
            nc.sync.dma_start(
                out=w2_sc[32 * q : 32 * q + 4, :].bitcast(I32),
                in_=w2_scales[0, 4 * q : 4 * q + 4, :].bitcast(I32),
            )

        ident = keep.tile([P, P], F32, name="ident")
        make_identity(nc, ident[:])
        bias = keep.tile([P, M], F32, name="bias")
        bias_v = bias[:].rearrange("p (n u c) -> p u n c", u=2, c=4)
        for u in range(2):
            bank = psum.tile([P, 512], F32, name="bank")
            for c in range(4):
                column = b_col[:, 4 * u + c : 4 * u + c + 1].to_broadcast([P, P])
                nc.tensor.transpose(bank[:, 128 * c : 128 * c + 128], column, ident[:])
            nc.scalar.activation(bias_v[:, u], bank[:].rearrange("p (c n) -> p n c", c=4), COPY)

        x_scales = []

        def gather_scales(g):
            scales = keep.tile([P, 256], U8, name=f"x_scales{g}", align_bytes=64)
            nc.vector.tensor_copy(scales[:], tab_scales[:].indirect(offsets[:, 16 * g : 16 * g + 16]))
            x_scales.append(scales)

        w1_bf = keep.tile([P, 4 * H], BF16, name="w1_bf", align_bytes=64)
        w1_dst = w1_bf[:].rearrange("p (t m j) -> p m t j", t=4, j=4)
        w1_src = w1_raw[:].rearrange("p j (m t) -> p m t j", t=4)
        nc.vector.tensor_copy(out=w1_dst[:, :W1_VECTOR], in_=w1_src[:, :W1_VECTOR])
        nc.scalar.activation(w1_dst[:, W1_VECTOR:], w1_src[:, W1_VECTOR:], COPY)
        w1_codes = keep.tile([P, H], U32, name="w1_codes", align_bytes=64)
        w1_sc = keep.tile([P, H], U8, name="w1_sc", align_bytes=64)
        gather_scales(0)
        nc.vector.quantize_mx(out=w1_codes[:].bitcast(FP8X4), scales=w1_sc[:], in_=w1_bf[:])

        x_words = []
        for g in range(2):
            words = keep.tile([P, 256], U32, name=f"x_words{g}", align_bytes=64)
            nc.vector.tensor_copy(words[:], tab_words[:].indirect(offsets[:, 16 * g : 16 * g + 16]))
            x_words.append(words)

        gather_scales(1)

        h_banks, h_codes = [], []

        def first_product(c):
            bank = psum.tile([P, 512], F32, name="bank")
            cols = slice(128 * (c % 2), 128 * (c % 2) + 128)
            for t in range(4):
                r = slice(128 * t, 128 * t + 128)
                nc.tensor.matmul_mx(
                    out=bank[:, r],
                    lhsT=w1_codes[:, r].bitcast(FP8X4),
                    lhsT_scale=w1_sc[:, r],
                    rhs=x_words[c // 2][:, cols].bitcast(FP8X4),
                    rhs_scale=x_scales[c // 2][:, cols],
                    start=True,
                    stop=True,
                )
            h_bf = ring.tile([P, 512], BF16, name="h_bf", align_bytes=64)
            nc.scalar.activation(
                h_bf[:].rearrange("p (n t) -> p n t", t=4), bank[:].rearrange("p (t n) -> p n t", t=4), RELU
            )
            h_banks.append(h_bf)

        def quantise(c):
            codes = ring.tile([P, 128], U32, name="h_codes", align_bytes=64)
            scales = ring.tile([P, 128], U8, name="h_scales", align_bytes=64)
            nc.vector.quantize_mx(out=codes[:].bitcast(FP8X4), scales=scales[:], in_=h_banks[c][:])
            h_codes.append((codes, scales))

        def second_product(c, n0, width, on_gpsimd=False):
            codes, scales = h_codes[c]
            bank = psum.tile([P, 512], F32, name="bank")
            cols = slice(n0, n0 + width)
            nc.tensor.matmul_mx(
                out=bank[:, :width],
                lhsT=codes[:].bitcast(FP8X4),
                lhsT_scale=scales[:],
                rhs=w2_codes[:, 2 * n0 : 2 * (n0 + width)].bitcast(FP4X4),
                rhs_scale=w2_sc[:, cols],
                start=True,
                stop=True,
            )
            result = outs.tile([P, 512], F32, name="result")
            if on_gpsimd:
                nc.scalar.activation(result[:, :width], bank[:, :width], COPY)
                nc.gpsimd.tensor_tensor(result[:, :width], result[:, :width], bias[:, cols], ADD)
            else:
                nc.vector.tensor_tensor(result[:, :width], bank[:, :width], bias[:, cols], ADD)
            nc.sync.dma_start(out=out[128 * c : 128 * c + 128, cols], in_=result[:, :width])

        first_product(0)
        first_product(1)
        quantise(0)
        second_product(0, 0, 256)
        second_product(0, 256, 256)
        first_product(2)
        quantise(1)
        second_product(0, 512, 512, on_gpsimd=True)
        first_product(3)
        second_product(1, 0, 512)
        quantise(2)
        second_product(1, 512, 512)
        second_product(2, 0, 512)
        quantise(3)
        second_product(2, 512, 512, on_gpsimd=True)
        second_product(3, 0, 512)
        second_product(3, 512, 512)
